import numpy as np
import ml_dtypes


def mxq(x, axis, fmt="e4m3"):
    dtype, down = {"e4m3": (ml_dtypes.float8_e4m3fn, 7), "e5m2": (ml_dtypes.float8_e5m2, 14)}[fmt]
    v = np.moveaxis(np.asarray(x, np.float32).astype(ml_dtypes.bfloat16).astype(np.float64), axis, -1)
    blocks = v.reshape(v.shape[:-1] + (-1, 32))
    amax = np.abs(blocks).max(-1, keepdims=True)
    byte = np.maximum(np.where(amax > 0, np.frexp(amax)[1] - 1 + 127, 0) - down, 1)
    scale = np.exp2(byte - 127.0)
    codes = (blocks / scale).astype(np.float32).astype(dtype).astype(np.float64)
    return np.moveaxis((codes * scale).reshape(v.shape), -1, axis)


WIDE = False


def mx_kscale(k):
    if not WIDE:
        return np.ones(k)
    levels = np.array([10, -10, 5, -5, 0])
    if k % 512:
        return np.exp2(np.random.permutation(np.resize(levels, k // 32))).repeat(32)
    a = np.empty((k // 512, 16))
    for p in range(k // 512):
        a[p, :8] = np.random.permutation(np.resize(levels, 8))
        for g in range(8):
            far = levels[np.abs(levels - a[p, g]) >= 10]
            a[p, g + 8] = far[np.random.randint(len(far))]
    return np.exp2(a.ravel()).repeat(32)


def f64(x):
    return np.asarray(x).astype(np.float64)


def striped(idx):
    return np.tile(np.asarray(idx).reshape(-1, 16).T, (8, 1)).astype(np.uint16)


def unstriped(offs):
    return offs[:16].T.reshape(-1).astype(np.int64)


E2M1 = np.array([0.0, 0.5, 1.0, 1.5, 2.0, 3.0, 4.0, 6.0, -0.0, -0.5, -1.0, -1.5, -2.0, -3.0, -4.0, -6.0])


def pack_weight(w, fmt):
    k, n = w.shape
    w = f64(np.asarray(w, np.float32).astype(ml_dtypes.bfloat16)).reshape(k // 32, 32, n)
    amax = np.abs(w).max(1)
    if fmt == "e4m3":
        byte = np.frexp(amax)[1] - 1 + 127 - 7
    else:
        mant, ex = np.frexp(amax / 6.0)
        byte = np.where(mant > 0.5, ex, ex - 1) + 127
    byte = np.clip(np.where(amax > 0, byte, 1), 1, 254)
    scaled = (w * np.exp2(127.0 - byte)[:, None, :]).reshape(k, n).astype(np.float32)
    by_word = np.ascontiguousarray(scaled.reshape(k // 512, 128, 4, n).transpose(0, 1, 3, 2))
    if fmt == "e4m3":
        words = by_word.astype(ml_dtypes.float8_e4m3fn).view(np.uint8)
    else:
        c = by_word.astype(ml_dtypes.float4_e2m1fn).view(np.uint8) & 0xF
        words = (c[..., 0::2] | (c[..., 1::2] << 4)).reshape(k // 512, 128, 2 * n)
    return np.ascontiguousarray(words), np.ascontiguousarray(byte.astype(np.uint8).reshape(k // 512, 16, n))


def unpack_weight(words, scales, fmt):
    g, _, n = scales.shape
    words = np.ascontiguousarray(words).reshape(g, 128, n, -1)
    if fmt == "e4m3":
        vals = words.view(ml_dtypes.float8_e4m3fn).astype(np.float64)
    else:
        nib = np.empty((g, 128, n, 4), np.uint8)
        nib[..., 0::2] = words & 0xF
        nib[..., 1::2] = words >> 4
        vals = E2M1[nib]
    vals = vals * np.repeat(np.exp2(scales.astype(np.float64) - 127.0), 8, axis=1)[..., None]
    return vals.transpose(0, 1, 3, 2).reshape(g * 512, n)


def bf(x):
    return np.asarray(x, np.float32).astype(ml_dtypes.bfloat16)


def planes(Y):
    r, m = Y.shape
    b = f64(bf(Y)).reshape(r // 32, 32, m)
    amax = np.abs(b).max(1)
    byte = np.clip(np.where(amax > 0, np.frexp(amax)[1] - 1 + 127 - 7, 1), 1, 254)
    codes = (b * np.exp2(127.0 - byte)[:, None, :]).reshape(r, m).astype(np.float32).astype(ml_dtypes.float8_e4m3fn).view(np.uint8)
    words = codes.reshape(r // 512, 128, 4, m).transpose(0, 1, 3, 2)
    return np.ascontiguousarray(words), np.ascontiguousarray(byte.astype(np.uint8).reshape(r // 512, 16, m))


D, T, I, Q, E, M = 512, 2048, 512, 256, 512, 1024


def setup_inputs():
    n = np.random.standard_normal
    idx = np.random.permutation(T)[:I]
    idx2 = np.random.permutation(T)[:I]
    idx3 = np.random.permutation(M)[:Q]
    fd = mx_kscale(D)
    fi = mx_kscale(I)
    ti = np.ones(T)
    ti[idx] = fi
    keysp = pack_weight(n((D, T)) / fd[:, None], "e2m1")
    return {
        "query": (n((D, Q)) * 1.0 / np.sqrt(D) * fd[:, None]).astype(np.float32),
        "keys_words": keysp[0],
        "keys_scales": keysp[1],
        "os": (np.random.uniform(0.02, 0.08, (1, I)) * fi).astype(np.float32),
        "vals": (n((E, T)) / ti).astype(np.float32),
        "member": (n((E, M))).astype(np.float32),
        "offs": striped(idx),
        "offs2": striped(idx2),
        "offs3": striped(idx3),
    }


def reference(query, keys_words, keys_scales, os, vals, member, offs, offs2, offs3):
    idx = unstriped(offs)
    idx2 = unstriped(offs2)
    idx3 = unstriped(offs3)
    keysu = unpack_weight(keys_words, keys_scales, "e2m1")
    queryq = mxq(f64(query), 0, "e4m3")
    a = queryq.T @ keysu
    s = a[:, idx] - a[:, idx2]
    w = np.maximum(s, 0.0)
    wo1 = w * f64(os)
    wt1 = wo1.T
    vt1 = f64(vals)[:, idx].T
    vt1q = mxq(vt1, 0, "e4m3")
    wt1q = mxq(wt1, 0, "e4m3")
    o = vt1q.T @ wt1q
    y = np.abs(o - f64(member)[:, idx3])
    words, scales = planes(y)
    return y, words, scales

@@ -1,0 +1,257 @@
+from contextlib import ExitStack
+
+import concourse.mybir as mybir
+from concourse.masks import make_identity
+
+D, T, I, Q, E, M = 512, 2048, 512, 256, 512, 1024
+FLOPS = 2 * D * Q * T + 2 * I * E * Q
+
+F32 = mybir.dt.float32
+BF16 = mybir.dt.bfloat16
+I32 = mybir.dt.int32
+U32 = mybir.dt.uint32
+U16 = mybir.dt.uint16
+U8 = mybir.dt.uint8
+FP8X4 = mybir.dt.float8_e4m3fn_x4
+FP4X4 = mybir.dt.float4_e2m1fn_x4
+ALU = mybir.AluOpType
+ACT = mybir.ActivationFunctionType
+
+P = 128
+PACK = 4
+BANK = 512
+QB = Q // P
+
+
+def tile_attend_difference_distanceout_lean_pl_kernel(
+    tc, query, keys_words, keys_scales, slot_factor, vals, member, offs, offs2, offs3, out_0, out_1, out_2
+):
+    nc = tc.nc
+    with ExitStack() as ctx:
+        lists = ctx.enter_context(tc.tile_pool(name="lists", bufs=1))
+        sb = ctx.enter_context(tc.tile_pool(name="sb", bufs=1))
+        ps = ctx.enter_context(tc.psum_pool(name="ps", bufs=6))
+        ps_v = ctx.enter_context(tc.psum_pool(name="ps_v", bufs=2))
+
+        q_raw = sb.tile([P, PACK, Q], F32, name="q_raw")
+        nc.sync.dma_start(out=q_raw[:], in_=query.rearrange("(p j) q -> p j q", j=PACK))
+
+        k_scale = sb.tile([P, T], U8, name="k_scale", align_bytes=64)
+        nc.gpsimd.memset(k_scale[:].bitcast(I32), 0)
+        for quad in range(4):
+            nc.sync.dma_start(
+                out=k_scale[32 * quad : 32 * quad + 4, :].bitcast(I32),
+                in_=keys_scales[0, 4 * quad : 4 * quad + 4, :].bitcast(I32),
+            )
+        k_words = sb.tile([P, 2 * T], U8, name="k_words", align_bytes=64)
+        nc.sync.dma_start(out=k_words[:].bitcast(I32), in_=keys_words[0].bitcast(I32))
+
+        vals_planes = vals.rearrange("(p j) t -> j p t", j=PACK)
+        member_planes = member.rearrange("(p j) m -> j p m", j=PACK)
+        v_win = [sb.tile([P, T], F32, name="v_win%d" % j, tag="v_win%d" % j) for j in range(PACK)]
+        m_win = [sb.tile([P, M], F32, name="m_win%d" % j, tag="m_win%d" % j, align_bytes=64) for j in range(PACK)]
+        idx2 = lists.tile([P, I // 16], U16, name="idx2")
+        nc.sync.dma_start(idx2[:], offs2)
+        nc.sync.dma_start(out=v_win[0][:], in_=vals_planes[0])
+        idx = lists.tile([P, I // 16], U16, name="idx")
+        nc.sync.dma_start(idx[:], offs)
+        nc.sync.dma_start(out=v_win[1][:], in_=vals_planes[1])
+        os4 = sb.tile([P, PACK], F32, name="os4")
+        nc.sync.dma_start(out=os4[:], in_=slot_factor.rearrange("o (p t) -> (o p) t", t=PACK))
+        idx3 = lists.tile([P, Q // 16], U16, name="idx3")
+        nc.sync.dma_start(idx3[:], offs3)
+        for j in range(2, PACK):
+            nc.sync.dma_start(out=v_win[j][:], in_=vals_planes[j])
+        for j in range(PACK):
+            nc.sync.dma_start(out=m_win[j][:], in_=member_planes[j])
+
+        ident = sb.tile([P, P], F32, name="ident")
+        make_identity(nc, ident[:])
+
+        q_bf = [sb.tile([P, P, PACK], BF16, name="q_bf%d" % b, align_bytes=64) for b in range(QB)]
+        q_code = [sb.tile([P, P], U32, name="q_code%d" % b, align_bytes=64) for b in range(QB)]
+        q_scale = [sb.tile([P, P], U8, name="q_scale%d" % b, align_bytes=64) for b in range(QB)]
+
+        def weave_views(dst, src):
+            return (
+                dst.rearrange("p (c i) t -> p c t i", i=4),
+                src.rearrange("p t (c i) -> p c t i", i=4),
+            )
+
+        dst, src = weave_views(q_bf[0][:], q_raw[:, :, 0:P])
+        nc.vector.tensor_copy(out=dst, in_=src)
+        dst, src = weave_views(q_bf[1][:], q_raw[:, :, P : 2 * P])
+        nc.scalar.activation(out=dst, in_=src, func=ACT.Copy)
+        for b in range(QB):
+            nc.vector.quantize_mx(
+                out=q_code[b][:].bitcast(FP8X4),
+                scales=q_scale[b][:],
+                in_=q_bf[b][:].rearrange("p c t -> p (c t)"),
+            )
+
+        a_win = [sb.tile([P, T], F32, name="a_win%d" % b) for b in range(QB)]
+
+        def score_bank(b, n):
+            acc = ps.tile([P, BANK], F32, name="acc", tag="bank")
+            nc.tensor.matmul_mx(
+                out=acc[:],
+                lhsT=q_code[b][:].bitcast(FP8X4),
+                lhsT_scale=q_scale[b][:],
+                rhs=k_words[:, 2 * BANK * n : 2 * BANK * (n + 1)].bitcast(FP4X4),
+                rhs_scale=k_scale[:, n * BANK : (n + 1) * BANK],
+                start=True,
+                stop=True,
+            )
+            dst = a_win[b][:, n * BANK : (n + 1) * BANK]
+            if (b, n) not in ((0, 1), (0, 3)):
+                nc.scalar.activation(out=dst, in_=acc[:], func=ACT.Copy)
+            else:
+                nc.vector.tensor_copy(out=dst, in_=acc[:])
+
+        second = [sb.tile([P, I], F32, name="second%d" % b, tag="second%d" % b, align_bytes=64) for b in range(QB)]
+        diff = {}
+
+        def look_up_second(b):
+            if b == 0:
+                nc.vector.tensor_copy(second[b][:], a_win[b][:].indirect(idx2[:]))
+            else:
+                nc.scalar.activation(out=second[b][:], in_=a_win[b][:].indirect(idx2[:]), func=ACT.Copy)
+
+        def difference(b, tag):
+            diff[b] = sb.tile([P, I], F32, name="diff%d" % b, tag=tag)
+            nc.vector.tensor_tensor(diff[b][:], a_win[b][:].indirect(idx[:]), second[b][:], ALU.subtract)
+
+        w_code = sb.tile([P, Q], U32, name="w_code", align_bytes=64)
+        w_scale = sb.tile([P, Q], U8, name="w_scale", align_bytes=64)
+
+        def turn_scores(b):
+            turned = ps.tile([P, PACK, P], F32, name="turned", tag="bank")
+            for t in range(PACK):
+                nc.tensor.transpose(turned[:, t, :], diff[b][:, t::PACK], ident[:])
+            return turned
+
+        def weights(b, turned, w_bf):
+            nc.vector.scalar_tensor_tensor(
+                out=w_bf.rearrange("p (q t) -> p q t", t=PACK),
+                in0=turned[:].rearrange("p t q -> p q t"),
+                scalar=0.0,
+                in1=os4[:].unsqueeze(1).to_broadcast([P, P, PACK]),
+                op0=ALU.max,
+                op1=ALU.mult,
+            )
+            nc.vector.quantize_mx(
+                out=w_code[:, b * P : (b + 1) * P].bitcast(FP8X4),
+                scales=w_scale[:, b * P : (b + 1) * P],
+                in_=w_bf,
+            )
+
+        v_got = [sb.tile([P, I], BF16, name="v_got%d" % j, tag="v_got%d" % j, align_bytes=64) for j in range(PACK)]
+
+        def gather_vals(j):
+            if j == 0:
+                nc.vector.tensor_copy(v_got[j][:], v_win[j][:].indirect(idx[:]))
+            else:
+                nc.scalar.activation(out=v_got[j][:], in_=v_win[j][:].indirect(idx[:]), func=ACT.Copy)
+
+        v_code = {}
+        v_scale = [sb.tile([P, 2 * P], U8, name="v_scale%d" % g, align_bytes=64) for g in range(2)]
+
+        def turn_vals(g):
+            vt = ps_v.tile([P, 2, 2, P], F32, name="vt")
+            for jj in range(2):
+                pairs = v_got[2 * g + jj][:].bitcast(F32)
+                for u in range(2):
+                    nc.tensor.transpose(vt[:, jj, u, :], pairs[:, u::2], ident[:])
+            return vt
+
+        def quantise_vals(g, vt, bf_tag, code_tag):
+            v_bf_tile = sb.tile([P, 2 * I], BF16, name="v_bf%d" % g, tag=bf_tag, align_bytes=64)
+            v_bf = v_bf_tile[:]
+            dst = v_bf.bitcast(F32).rearrange("p (j m u) -> p j m u", j=2, u=2)
+            src = vt[:].rearrange("p j u m -> p j m u")
+            if g == 0:
+                nc.vector.tensor_copy(out=dst, in_=src)
+            else:
+                nc.scalar.copy(out=dst, in_=src)
+            v_code[g] = sb.tile([P, 2 * P], U32, name="v_code%d" % g, tag=code_tag, align_bytes=64)
+            nc.vector.quantize_mx(out=v_code[g][:].bitcast(FP8X4), scales=v_scale[g][:], in_=v_bf)
+
+        m_got = [sb.tile([P, 2 * Q], F32, name="m_got%d" % g) for g in range(2)]
+
+        def gather_member(j):
+            dst = m_got[j // 2][:, (j % 2) * Q : (j % 2 + 1) * Q]
+            if j == 1:
+                nc.vector.tensor_copy(dst, m_win[j][:].indirect(idx3[:]))
+            else:
+                nc.scalar.activation(out=dst, in_=m_win[j][:].indirect(idx3[:]), func=ACT.Copy)
+
+        for b in range(QB):
+            for n in range(4):
+                score_bank(b, n)
+        look_up_second(0)
+        difference(0, "diff0")
+        look_up_second(1)
+        gather_vals(0)
+        difference(1, "v_win0")
+        turned0 = turn_scores(0)
+        turned1 = turn_scores(1)
+        w_bf0 = sb.tile([P, I], BF16, name="w_bf0", tag="second1", align_bytes=64)
+        weights(0, turned0, w_bf0[:])
+        w_bf1 = sb.tile([P, I], BF16, name="w_bf1", align_bytes=64)
+        weights(1, turned1, w_bf1[:])
+        for j in range(1, PACK):
+            gather_vals(j)
+        vt0 = turn_vals(0)
+        vt1 = turn_vals(1)
+        gather_member(0)
+        quantise_vals(0, vt0, "v_bf0", "v_got3")
+        gather_member(1)
+        quantise_vals(1, vt1, "m_win0", "m_win1")
+        gather_member(2)
+        gather_member(3)
+
+        y = sb.tile([P, PACK, Q], F32, name="y", tag="m_win3", align_bytes=64)
+        gap = sb.tile([P, PACK * Q], F32, name="gap")
+        y_out = out_0.rearrange("(p j) q -> p j q", j=PACK)
+        o_acc = []
+        for g in range(2):
+            acc = ps.tile([P, 2 * Q], F32, name="o_acc", tag="bank")
+            for jj in range(2):
+                nc.tensor.matmul_mx(
+                    out=acc[:, jj * Q : (jj + 1) * Q],
+                    lhsT=v_code[g][:, jj * P : (jj + 1) * P].bitcast(FP8X4),
+                    lhsT_scale=v_scale[g][:, jj * P : (jj + 1) * P],
+                    rhs=w_code[:].bitcast(FP8X4),
+                    rhs_scale=w_scale[:],
+                    start=True,
+                    stop=True,
+                )
+            o_acc.append(acc)
+        y_flat = y[:].rearrange("p j q -> p (j q)")
+        for first, last in ((0, 2), (2, 3), (3, 4)):
+            g = first // 2
+            cols = slice(first * Q, last * Q)
+            local = slice((first - 2 * g) * Q, (last - 2 * g) * Q)
+            nc.vector.tensor_tensor(gap[:, cols], o_acc[g][:, local], m_got[g][:, local], ALU.subtract)
+            nc.scalar.activation(out=y_flat[:, cols], in_=gap[:, cols], func=ACT.Abs)
+            if last == PACK - 1:
+                nc.sync.dma_start(out=y_out[:, 0 : PACK - 1, :], in_=y[:, 0 : PACK - 1, :])
+        nc.scalar.dma_start(out=y_out[:, PACK - 1, :], in_=y[:, PACK - 1, :])
+
+        y_bf = sb.tile([P, Q, PACK], BF16, name="y_bf", align_bytes=64)
+        dst, src = weave_views(y_bf[:], y[:])
+        nc.vector.tensor_copy(out=dst, in_=src)
+        y_code = sb.tile([P, Q], U32, name="y_code", align_bytes=64)
+        y_scale = sb.tile([P, Q], U8, name="y_scale", align_bytes=64)
+        nc.vector.quantize_mx(
+            out=y_code[:].bitcast(FP8X4), scales=y_scale[:], in_=y_bf[:].rearrange("p c t -> p (c t)")
+        )
+        nc.sync.dma_start(
+            out=out_1[0].rearrange("p c r -> p (c r)").bitcast(I32), in_=y_code[:].bitcast(I32)
+        )
+        for quad in range(4):
+            queue = nc.scalar if quad % 2 == 0 else nc.sync
+            queue.dma_start(
+                out=out_2[0, 4 * quad : 4 * quad + 4, :].bitcast(I32),
+                in_=y_scale[32 * quad : 32 * quad + 4, :].bitcast(I32),
+            )

@@ -43,25 +43,28 @@ def tile_attend_difference_distanceout_lean_pl_kernel(
                 out=k_scale[32 * quad : 32 * quad + 4, :].bitcast(I32),
                 in_=keys_scales[0, 4 * quad : 4 * quad + 4, :].bitcast(I32),
             )
-        k_words = sb.tile([P, 2 * T], U8, name="k_words", align_bytes=64)
-        nc.sync.dma_start(out=k_words[:].bitcast(I32), in_=keys_words[0].bitcast(I32))
+        k_words = [sb.tile([P, T], U8, name="k_words%d" % h, align_bytes=64) for h in range(2)]
+        for h in range(2):
+            nc.sync.dma_start(
+                out=k_words[h][:].bitcast(I32), in_=keys_words[0, :, h * T : (h + 1) * T].bitcast(I32)
+            )
 
         vals_planes = vals.rearrange("(p j) t -> j p t", j=PACK)
         member_planes = member.rearrange("(p j) m -> j p m", j=PACK)
-        v_win = [sb.tile([P, T], F32, name="v_win%d" % j, tag="v_win%d" % j) for j in range(PACK)]
+        v_win = [sb.tile([P, T], F32, name="v_win%d" % j, tag="v_win%d" % j, align_bytes=64) for j in range(PACK)]
         m_win = [sb.tile([P, M], F32, name="m_win%d" % j, tag="m_win%d" % j, align_bytes=64) for j in range(PACK)]
         idx2 = lists.tile([P, I // 16], U16, name="idx2")
-        nc.sync.dma_start(idx2[:], offs2)
         nc.sync.dma_start(out=v_win[0][:], in_=vals_planes[0])
+        nc.sync.dma_start(idx2[:], offs2)
+        nc.sync.dma_start(out=v_win[1][:], in_=vals_planes[1])
         idx = lists.tile([P, I // 16], U16, name="idx")
         nc.sync.dma_start(idx[:], offs)
-        nc.sync.dma_start(out=v_win[1][:], in_=vals_planes[1])
         os4 = sb.tile([P, PACK], F32, name="os4")
         nc.sync.dma_start(out=os4[:], in_=slot_factor.rearrange("o (p t) -> (o p) t", t=PACK))
-        idx3 = lists.tile([P, Q // 16], U16, name="idx3")
-        nc.sync.dma_start(idx3[:], offs3)
         for j in range(2, PACK):
             nc.sync.dma_start(out=v_win[j][:], in_=vals_planes[j])
+        idx3 = lists.tile([P, Q // 16], U16, name="idx3")
+        nc.sync.dma_start(idx3[:], offs3)
         for j in range(PACK):
             nc.sync.dma_start(out=m_win[j][:], in_=member_planes[j])
 
@@ -97,13 +100,13 @@ def tile_attend_difference_distanceout_lean_pl_kernel(
                 out=acc[:],
                 lhsT=q_code[b][:].bitcast(FP8X4),
                 lhsT_scale=q_scale[b][:],
-                rhs=k_words[:, 2 * BANK * n : 2 * BANK * (n + 1)].bitcast(FP4X4),
+                rhs=k_words[n // 2][:, 2 * BANK * (n % 2) : 2 * BANK * (n % 2 + 1)].bitcast(FP4X4),
                 rhs_scale=k_scale[:, n * BANK : (n + 1) * BANK],
                 start=True,
                 stop=True,
             )
             dst = a_win[b][:, n * BANK : (n + 1) * BANK]
-            if (b, n) not in ((0, 1), (0, 3)):
+            if (b, n) in ((0, 0), (0, 2), (1, 0)):
                 nc.scalar.activation(out=dst, in_=acc[:], func=ACT.Copy)
             else:
                 nc.vector.tensor_copy(out=dst, in_=acc[:])
@@ -112,16 +115,12 @@ def tile_attend_difference_distanceout_lean_pl_kernel(
         diff = {}
 
         def look_up_second(b):
-            if b == 0:
-                nc.vector.tensor_copy(second[b][:], a_win[b][:].indirect(idx2[:]))
-            else:
-                nc.scalar.activation(out=second[b][:], in_=a_win[b][:].indirect(idx2[:]), func=ACT.Copy)
+            nc.scalar.activation(out=second[b][:], in_=a_win[b][:].indirect(idx2[:]), func=ACT.Copy)
 
         def difference(b, tag):
             diff[b] = sb.tile([P, I], F32, name="diff%d" % b, tag=tag)
             nc.vector.tensor_tensor(diff[b][:], a_win[b][:].indirect(idx[:]), second[b][:], ALU.subtract)
 
-        w_code = sb.tile([P, Q], U32, name="w_code", align_bytes=64)
         w_scale = sb.tile([P, Q], U8, name="w_scale", align_bytes=64)
 
         def turn_scores(b):
@@ -139,11 +138,6 @@ def tile_attend_difference_distanceout_lean_pl_kernel(
                 op0=ALU.max,
                 op1=ALU.mult,
             )
-            nc.vector.quantize_mx(
-                out=w_code[:, b * P : (b + 1) * P].bitcast(FP8X4),
-                scales=w_scale[:, b * P : (b + 1) * P],
-                in_=w_bf,
-            )
 
         v_got = [sb.tile([P, I], BF16, name="v_got%d" % j, tag="v_got%d" % j, align_bytes=64) for j in range(PACK)]
 
@@ -153,70 +147,78 @@ def tile_attend_difference_distanceout_lean_pl_kernel(
             else:
                 nc.scalar.activation(out=v_got[j][:], in_=v_win[j][:].indirect(idx[:]), func=ACT.Copy)
 
-        v_code = {}
-        v_scale = [sb.tile([P, 2 * P], U8, name="v_scale%d" % g, align_bytes=64) for g in range(2)]
+        groups = ((0, 1), (2,), (3,))
+        v_code = [sb.tile([P, len(g) * P], U32, name="v_code%d" % g[0], align_bytes=64) for g in groups]
+        v_scale = [sb.tile([P, len(g) * P], U8, name="v_scale%d" % g[0], align_bytes=64) for g in groups]
+        v_bf = {}
 
         def turn_vals(g):
-            vt = ps_v.tile([P, 2, 2, P], F32, name="vt")
-            for jj in range(2):
-                pairs = v_got[2 * g + jj][:].bitcast(F32)
+            vt = ps_v.tile([P, len(groups[g]), 2, P], F32, name="vt")
+            for jj, j in enumerate(groups[g]):
+                pairs = v_got[j][:].bitcast(F32)
                 for u in range(2):
                     nc.tensor.transpose(vt[:, jj, u, :], pairs[:, u::2], ident[:])
             return vt
 
-        def quantise_vals(g, vt, bf_tag, code_tag):
-            v_bf_tile = sb.tile([P, 2 * I], BF16, name="v_bf%d" % g, tag=bf_tag, align_bytes=64)
-            v_bf = v_bf_tile[:]
-            dst = v_bf.bitcast(F32).rearrange("p (j m u) -> p j m u", j=2, u=2)
+        def weave_vals(g, vt, tag):
+            v_bf[g] = sb.tile([P, len(groups[g]) * I], BF16, name="v_bf%d" % g, tag=tag, align_bytes=64)
+            dst = v_bf[g][:].bitcast(F32).rearrange("p (j m u) -> p j m u", m=P, u=2)
             src = vt[:].rearrange("p j u m -> p j m u")
-            if g == 0:
+            if g < 2:
                 nc.vector.tensor_copy(out=dst, in_=src)
             else:
                 nc.scalar.copy(out=dst, in_=src)
-            v_code[g] = sb.tile([P, 2 * P], U32, name="v_code%d" % g, tag=code_tag, align_bytes=64)
-            nc.vector.quantize_mx(out=v_code[g][:].bitcast(FP8X4), scales=v_scale[g][:], in_=v_bf)
 
-        m_got = [sb.tile([P, 2 * Q], F32, name="m_got%d" % g) for g in range(2)]
+        def quantise_vals(g):
+            nc.vector.quantize_mx(out=v_code[g][:].bitcast(FP8X4), scales=v_scale[g][:], in_=v_bf[g][:])
+
+        m_got = sb.tile([P, (PACK - 1) * Q], F32, name="m_got")
 
         def gather_member(j):
-            dst = m_got[j // 2][:, (j % 2) * Q : (j % 2 + 1) * Q]
-            if j == 1:
-                nc.vector.tensor_copy(dst, m_win[j][:].indirect(idx3[:]))
-            else:
-                nc.scalar.activation(out=dst, in_=m_win[j][:].indirect(idx3[:]), func=ACT.Copy)
+            nc.scalar.activation(
+                out=m_got[:, j * Q : (j + 1) * Q], in_=m_win[j][:].indirect(idx3[:]), func=ACT.Copy
+            )
 
         for b in range(QB):
             for n in range(4):
                 score_bank(b, n)
         look_up_second(0)
-        difference(0, "diff0")
         look_up_second(1)
+        difference(0, "diff0")
         gather_vals(0)
-        difference(1, "v_win0")
-        turned0 = turn_scores(0)
-        turned1 = turn_scores(1)
-        w_bf0 = sb.tile([P, I], BF16, name="w_bf0", tag="second1", align_bytes=64)
-        weights(0, turned0, w_bf0[:])
-        w_bf1 = sb.tile([P, I], BF16, name="w_bf1", align_bytes=64)
-        weights(1, turned1, w_bf1[:])
+        difference(1, "diff1")
         for j in range(1, PACK):
             gather_vals(j)
+        turned0 = turn_scores(0)
         vt0 = turn_vals(0)
+        turned1 = turn_scores(1)
+        w_bf = sb.tile([P, QB * I], BF16, name="w_bf", align_bytes=64)
+        weights(0, turned0, w_bf[:, 0:I])
+        weave_vals(0, vt0, "v_bf0")
+        weights(1, turned1, w_bf[:, I : 2 * I])
+        quantise_vals(0)
         vt1 = turn_vals(1)
+        vt2 = turn_vals(2)
+        weave_vals(1, vt1, "v_bf1")
+        quantise_vals(1)
+        w_code = sb.tile([P, Q], U32, name="w_code", tag="v_win3", align_bytes=64)
+        nc.vector.quantize_mx(out=w_code[:].bitcast(FP8X4), scales=w_scale[:], in_=w_bf[:])
         gather_member(0)
-        quantise_vals(0, vt0, "v_bf0", "v_got3")
+        weave_vals(2, vt2, "m_win0")
+        quantise_vals(2)
         gather_member(1)
-        quantise_vals(1, vt1, "m_win0", "m_win1")
         gather_member(2)
-        gather_member(3)
 
-        y = sb.tile([P, PACK, Q], F32, name="y", tag="m_win3", align_bytes=64)
+        late = sb.tile([P, (PACK + 1) * Q], F32, name="late", tag="m_win2", align_bytes=64)
+        y_flat = late[:, 0 : PACK * Q]
+        y = y_flat.rearrange("p (j q) -> p j q", j=PACK)
+        o_last = late[:, PACK * Q : (PACK + 1) * Q]
         gap = sb.tile([P, PACK * Q], F32, name="gap")
         y_out = out_0.rearrange("(p j) q -> p j q", j=PACK)
         o_acc = []
-        for g in range(2):
-            acc = ps.tile([P, 2 * Q], F32, name="o_acc", tag="bank")
-            for jj in range(2):
+        for g, planes in enumerate(groups):
+            acc = ps.tile([P, len(planes) * Q], F32, name="o_acc", tag="bank")
+            for jj in range(len(planes)):
                 nc.tensor.matmul_mx(
                     out=acc[:, jj * Q : (jj + 1) * Q],
                     lhsT=v_code[g][:, jj * P : (jj + 1) * P].bitcast(FP8X4),
@@ -227,30 +229,53 @@ def tile_attend_difference_distanceout_lean_pl_kernel(
                     stop=True,
                 )
             o_acc.append(acc)
-        y_flat = y[:].rearrange("p j q -> p (j q)")
-        for first, last in ((0, 2), (2, 3), (3, 4)):
-            g = first // 2
-            cols = slice(first * Q, last * Q)
-            local = slice((first - 2 * g) * Q, (last - 2 * g) * Q)
-            nc.vector.tensor_tensor(gap[:, cols], o_acc[g][:, local], m_got[g][:, local], ALU.subtract)
-            nc.scalar.activation(out=y_flat[:, cols], in_=gap[:, cols], func=ACT.Abs)
-            if last == PACK - 1:
-                nc.sync.dma_start(out=y_out[:, 0 : PACK - 1, :], in_=y[:, 0 : PACK - 1, :])
-        nc.scalar.dma_start(out=y_out[:, PACK - 1, :], in_=y[:, PACK - 1, :])
 
-        y_bf = sb.tile([P, Q, PACK], BF16, name="y_bf", align_bytes=64)
-        dst, src = weave_views(y_bf[:], y[:])
-        nc.vector.tensor_copy(out=dst, in_=src)
+        nc.scalar.activation(out=o_last, in_=o_acc[2][:], func=ACT.Copy)
+        for g in range(2):
+            cols = slice(groups[g][0] * Q, (groups[g][-1] + 1) * Q)
+            nc.vector.tensor_tensor(gap[:, cols], o_acc[g][:], m_got[:, cols], ALU.subtract)
+            nc.scalar.activation(out=y_flat[:, cols], in_=gap[:, cols], func=ACT.Abs)
+        nc.sync.dma_start(out=y_out[:, 0 : PACK - 1, :], in_=y[:, 0 : PACK - 1, :])
+
+        y_bf = [sb.tile([P, P, PACK], BF16, name="y_bf%d" % b, align_bytes=64) for b in range(QB)]
         y_code = sb.tile([P, Q], U32, name="y_code", align_bytes=64)
         y_scale = sb.tile([P, Q], U8, name="y_scale", align_bytes=64)
-        nc.vector.quantize_mx(
-            out=y_code[:].bitcast(FP8X4), scales=y_scale[:], in_=y_bf[:].rearrange("p c t -> p (c t)")
-        )
-        nc.sync.dma_start(
+        halves = [slice(b * P, (b + 1) * P) for b in range(QB)]
+        for b in range(QB):
+            dst, src = weave_views(y_bf[b][:, :, 0:2], y[:, 0:2, halves[b]])
+            nc.scalar.activation(out=dst, in_=src, func=ACT.Copy)
+        gap_last = gap[:, (PACK - 1) * Q : PACK * Q]
+        for b in range(QB):
+            nc.vector.tensor_tensor(
+                gap_last[:, halves[b]],
+                m_win[PACK - 1][:].indirect(idx3[:, b * P // 16 : (b + 1) * P // 16]),
+                o_last[:, halves[b]],
+                ALU.subtract,
+            )
+        for b in range(QB):
+            nc.vector.scalar_tensor_tensor(
+                out=y[:, PACK - 1, halves[b]],
+                in0=gap_last[:, halves[b]],
+                scalar=-1.0,
+                in1=gap_last[:, halves[b]],
+                op0=ALU.mult,
+                op1=ALU.max,
+            )
+        nc.sync.dma_start(out=y_out[:, PACK - 1, :], in_=y[:, PACK - 1, :])
+        for b in range(QB):
+            dst, src = weave_views(y_bf[b][:, :, 2:4], y[:, 2:4, halves[b]])
+            nc.vector.tensor_copy(out=dst, in_=src)
+        for b in range(QB):
+            nc.vector.quantize_mx(
+                out=y_code[:, halves[b]].bitcast(FP8X4),
+                scales=y_scale[:, halves[b]],
+                in_=y_bf[b][:].rearrange("p c t -> p (c t)"),
+            )
+        nc.scalar.dma_start(
             out=out_1[0].rearrange("p c r -> p (c r)").bitcast(I32), in_=y_code[:].bitcast(I32)
         )
         for quad in range(4):
-            queue = nc.scalar if quad % 2 == 0 else nc.sync
+            queue = nc.scalar if quad == 3 else nc.sync
             queue.dma_start(
                 out=out_2[0, 4 * quad : 4 * quad + 4, :].bitcast(I32),
                 in_=y_scale[32 * quad : 32 * quad + 4, :].bitcast(I32),

from contextlib import ExitStack

import concourse.mybir as mybir
from concourse.masks import make_identity

D, T, I, Q, E, M = 512, 2048, 512, 256, 512, 1024
FLOPS = 2 * D * Q * T + 2 * I * E * Q

F32 = mybir.dt.float32
BF16 = mybir.dt.bfloat16
I32 = mybir.dt.int32
U32 = mybir.dt.uint32
U16 = mybir.dt.uint16
U8 = mybir.dt.uint8
FP8X4 = mybir.dt.float8_e4m3fn_x4
FP4X4 = mybir.dt.float4_e2m1fn_x4
ALU = mybir.AluOpType
ACT = mybir.ActivationFunctionType

P = 128
PACK = 4
BANK = 512
QB = Q // P


def tile_attend_difference_distanceout_lean_pl_kernel(
    tc, query, keys_words, keys_scales, slot_factor, vals, member, offs, offs2, offs3, out_0, out_1, out_2
):
    nc = tc.nc
    with ExitStack() as ctx:
        lists = ctx.enter_context(tc.tile_pool(name="lists", bufs=1))
        sb = ctx.enter_context(tc.tile_pool(name="sb", bufs=1))
        ps = ctx.enter_context(tc.psum_pool(name="ps", bufs=6))
        ps_v = ctx.enter_context(tc.psum_pool(name="ps_v", bufs=2))

        q_raw = sb.tile([P, PACK, Q], F32, name="q_raw")
        nc.sync.dma_start(out=q_raw[:], in_=query.rearrange("(p j) q -> p j q", j=PACK))

        k_scale = sb.tile([P, T], U8, name="k_scale", align_bytes=64)
        nc.gpsimd.memset(k_scale[:].bitcast(I32), 0)
        for quad in range(4):
            nc.sync.dma_start(
                out=k_scale[32 * quad : 32 * quad + 4, :].bitcast(I32),
                in_=keys_scales[0, 4 * quad : 4 * quad + 4, :].bitcast(I32),
            )
        k_words = [sb.tile([P, T], U8, name="k_words%d" % h, align_bytes=64) for h in range(2)]
        for h in range(2):
            nc.sync.dma_start(
                out=k_words[h][:].bitcast(I32), in_=keys_words[0, :, h * T : (h + 1) * T].bitcast(I32)
            )

        vals_planes = vals.rearrange("(p j) t -> j p t", j=PACK)
        member_planes = member.rearrange("(p j) m -> j p m", j=PACK)
        v_win = [sb.tile([P, T], F32, name="v_win%d" % j, tag="v_win%d" % j, align_bytes=64) for j in range(PACK)]
        m_win = [sb.tile([P, M], F32, name="m_win%d" % j, tag="m_win%d" % j, align_bytes=64) for j in range(PACK)]
        idx2 = lists.tile([P, I // 16], U16, name="idx2")
        nc.sync.dma_start(out=v_win[0][:], in_=vals_planes[0])
        nc.sync.dma_start(idx2[:], offs2)
        nc.sync.dma_start(out=v_win[1][:], in_=vals_planes[1])
        idx = lists.tile([P, I // 16], U16, name="idx")
        nc.sync.dma_start(idx[:], offs)
        os4 = sb.tile([P, PACK], F32, name="os4")
        nc.sync.dma_start(out=os4[:], in_=slot_factor.rearrange("o (p t) -> (o p) t", t=PACK))
        for j in range(2, PACK):
            nc.sync.dma_start(out=v_win[j][:], in_=vals_planes[j])
        idx3 = lists.tile([P, Q // 16], U16, name="idx3")
        nc.sync.dma_start(idx3[:], offs3)
        for j in range(PACK):
            nc.sync.dma_start(out=m_win[j][:], in_=member_planes[j])

        ident = sb.tile([P, P], F32, name="ident")
        make_identity(nc, ident[:])

        q_bf = [sb.tile([P, P, PACK], BF16, name="q_bf%d" % b, align_bytes=64) for b in range(QB)]
        q_code = [sb.tile([P, P], U32, name="q_code%d" % b, align_bytes=64) for b in range(QB)]
        q_scale = [sb.tile([P, P], U8, name="q_scale%d" % b, align_bytes=64) for b in range(QB)]

        def weave_views(dst, src):
            return (
                dst.rearrange("p (c i) t -> p c t i", i=4),
                src.rearrange("p t (c i) -> p c t i", i=4),
            )

        dst, src = weave_views(q_bf[0][:], q_raw[:, :, 0:P])
        nc.vector.tensor_copy(out=dst, in_=src)
        dst, src = weave_views(q_bf[1][:], q_raw[:, :, P : 2 * P])
        nc.scalar.activation(out=dst, in_=src, func=ACT.Copy)
        for b in range(QB):
            nc.vector.quantize_mx(
                out=q_code[b][:].bitcast(FP8X4),
                scales=q_scale[b][:],
                in_=q_bf[b][:].rearrange("p c t -> p (c t)"),
            )

        a_win = [sb.tile([P, T], F32, name="a_win%d" % b) for b in range(QB)]

        def score_bank(b, n):
            acc = ps.tile([P, BANK], F32, name="acc", tag="bank")
            nc.tensor.matmul_mx(
                out=acc[:],
                lhsT=q_code[b][:].bitcast(FP8X4),
                lhsT_scale=q_scale[b][:],
                rhs=k_words[n // 2][:, 2 * BANK * (n % 2) : 2 * BANK * (n % 2 + 1)].bitcast(FP4X4),
                rhs_scale=k_scale[:, n * BANK : (n + 1) * BANK],
                start=True,
                stop=True,
            )
            dst = a_win[b][:, n * BANK : (n + 1) * BANK]
            if (b, n) in ((0, 0), (0, 2), (1, 0)):
                nc.scalar.activation(out=dst, in_=acc[:], func=ACT.Copy)
            else:
                nc.vector.tensor_copy(out=dst, in_=acc[:])

        second = [sb.tile([P, I], F32, name="second%d" % b, tag="second%d" % b, align_bytes=64) for b in range(QB)]
        diff = {}

        def look_up_second(b):
            nc.scalar.activation(out=second[b][:], in_=a_win[b][:].indirect(idx2[:]), func=ACT.Copy)

        def difference(b, tag):
            diff[b] = sb.tile([P, I], F32, name="diff%d" % b, tag=tag)
            nc.vector.tensor_tensor(diff[b][:], a_win[b][:].indirect(idx[:]), second[b][:], ALU.subtract)

        w_scale = sb.tile([P, Q], U8, name="w_scale", align_bytes=64)

        def turn_scores(b):
            turned = ps.tile([P, PACK, P], F32, name="turned", tag="bank")
            for t in range(PACK):
                nc.tensor.transpose(turned[:, t, :], diff[b][:, t::PACK], ident[:])
            return turned

        def weights(b, turned, w_bf):
            nc.vector.scalar_tensor_tensor(
                out=w_bf.rearrange("p (q t) -> p q t", t=PACK),
                in0=turned[:].rearrange("p t q -> p q t"),
                scalar=0.0,
                in1=os4[:].unsqueeze(1).to_broadcast([P, P, PACK]),
                op0=ALU.max,
                op1=ALU.mult,
            )

        v_got = [sb.tile([P, I], BF16, name="v_got%d" % j, tag="v_got%d" % j, align_bytes=64) for j in range(PACK)]

        def gather_vals(j):
            if j == 0:
                nc.vector.tensor_copy(v_got[j][:], v_win[j][:].indirect(idx[:]))
            else:
                nc.scalar.activation(out=v_got[j][:], in_=v_win[j][:].indirect(idx[:]), func=ACT.Copy)

        groups = ((0, 1), (2,), (3,))
        v_code = [sb.tile([P, len(g) * P], U32, name="v_code%d" % g[0], align_bytes=64) for g in groups]
        v_scale = [sb.tile([P, len(g) * P], U8, name="v_scale%d" % g[0], align_bytes=64) for g in groups]
        v_bf = {}

        def turn_vals(g):
            vt = ps_v.tile([P, len(groups[g]), 2, P], F32, name="vt")
            for jj, j in enumerate(groups[g]):
                pairs = v_got[j][:].bitcast(F32)
                for u in range(2):
                    nc.tensor.transpose(vt[:, jj, u, :], pairs[:, u::2], ident[:])
            return vt

        def weave_vals(g, vt, tag):
            v_bf[g] = sb.tile([P, len(groups[g]) * I], BF16, name="v_bf%d" % g, tag=tag, align_bytes=64)
            dst = v_bf[g][:].bitcast(F32).rearrange("p (j m u) -> p j m u", m=P, u=2)
            src = vt[:].rearrange("p j u m -> p j m u")
            if g < 2:
                nc.vector.tensor_copy(out=dst, in_=src)
            else:
                nc.scalar.copy(out=dst, in_=src)

        def quantise_vals(g):
            nc.vector.quantize_mx(out=v_code[g][:].bitcast(FP8X4), scales=v_scale[g][:], in_=v_bf[g][:])

        m_got = sb.tile([P, (PACK - 1) * Q], F32, name="m_got")

        def gather_member(j):
            nc.scalar.activation(
                out=m_got[:, j * Q : (j + 1) * Q], in_=m_win[j][:].indirect(idx3[:]), func=ACT.Copy
            )

        for b in range(QB):
            for n in range(4):
                score_bank(b, n)
        look_up_second(0)
        look_up_second(1)
        difference(0, "diff0")
        gather_vals(0)
        difference(1, "diff1")
        for j in range(1, PACK):
            gather_vals(j)
        turned0 = turn_scores(0)
        vt0 = turn_vals(0)
        turned1 = turn_scores(1)
        w_bf = sb.tile([P, QB * I], BF16, name="w_bf", align_bytes=64)
        weights(0, turned0, w_bf[:, 0:I])
        weave_vals(0, vt0, "v_bf0")
        weights(1, turned1, w_bf[:, I : 2 * I])
        quantise_vals(0)
        vt1 = turn_vals(1)
        vt2 = turn_vals(2)
        weave_vals(1, vt1, "v_bf1")
        quantise_vals(1)
        w_code = sb.tile([P, Q], U32, name="w_code", tag="v_win3", align_bytes=64)
        nc.vector.quantize_mx(out=w_code[:].bitcast(FP8X4), scales=w_scale[:], in_=w_bf[:])
        gather_member(0)
        weave_vals(2, vt2, "m_win0")
        quantise_vals(2)
        gather_member(1)
        gather_member(2)

        late = sb.tile([P, (PACK + 1) * Q], F32, name="late", tag="m_win2", align_bytes=64)
        y_flat = late[:, 0 : PACK * Q]
        y = y_flat.rearrange("p (j q) -> p j q", j=PACK)
        o_last = late[:, PACK * Q : (PACK + 1) * Q]
        gap = sb.tile([P, PACK * Q], F32, name="gap")
        y_out = out_0.rearrange("(p j) q -> p j q", j=PACK)
        o_acc = []
        for g, planes in enumerate(groups):
            acc = ps.tile([P, len(planes) * Q], F32, name="o_acc", tag="bank")
            for jj in range(len(planes)):
                nc.tensor.matmul_mx(
                    out=acc[:, jj * Q : (jj + 1) * Q],
                    lhsT=v_code[g][:, jj * P : (jj + 1) * P].bitcast(FP8X4),
                    lhsT_scale=v_scale[g][:, jj * P : (jj + 1) * P],
                    rhs=w_code[:].bitcast(FP8X4),
                    rhs_scale=w_scale[:],
                    start=True,
                    stop=True,
                )
            o_acc.append(acc)

        nc.scalar.activation(out=o_last, in_=o_acc[2][:], func=ACT.Copy)
        for g in range(2):
            cols = slice(groups[g][0] * Q, (groups[g][-1] + 1) * Q)
            nc.vector.tensor_tensor(gap[:, cols], o_acc[g][:], m_got[:, cols], ALU.subtract)
            nc.scalar.activation(out=y_flat[:, cols], in_=gap[:, cols], func=ACT.Abs)
        nc.sync.dma_start(out=y_out[:, 0 : PACK - 1, :], in_=y[:, 0 : PACK - 1, :])

        y_bf = [sb.tile([P, P, PACK], BF16, name="y_bf%d" % b, align_bytes=64) for b in range(QB)]
        y_code = sb.tile([P, Q], U32, name="y_code", align_bytes=64)
        y_scale = sb.tile([P, Q], U8, name="y_scale", align_bytes=64)
        halves = [slice(b * P, (b + 1) * P) for b in range(QB)]
        for b in range(QB):
            dst, src = weave_views(y_bf[b][:, :, 0:2], y[:, 0:2, halves[b]])
            nc.scalar.activation(out=dst, in_=src, func=ACT.Copy)
        gap_last = gap[:, (PACK - 1) * Q : PACK * Q]
        for b in range(QB):
            nc.vector.tensor_tensor(
                gap_last[:, halves[b]],
                m_win[PACK - 1][:].indirect(idx3[:, b * P // 16 : (b + 1) * P // 16]),
                o_last[:, halves[b]],
                ALU.subtract,
            )
        for b in range(QB):
            nc.vector.scalar_tensor_tensor(
                out=y[:, PACK - 1, halves[b]],
                in0=gap_last[:, halves[b]],
                scalar=-1.0,
                in1=gap_last[:, halves[b]],
                op0=ALU.mult,
                op1=ALU.max,
            )
        nc.sync.dma_start(out=y_out[:, PACK - 1, :], in_=y[:, PACK - 1, :])
        for b in range(QB):
            dst, src = weave_views(y_bf[b][:, :, 2:4], y[:, 2:4, halves[b]])
            nc.vector.tensor_copy(out=dst, in_=src)
        for b in range(QB):
            nc.vector.quantize_mx(
                out=y_code[:, halves[b]].bitcast(FP8X4),
                scales=y_scale[:, halves[b]],
                in_=y_bf[b][:].rearrange("p c t -> p (c t)"),
            )
        nc.scalar.dma_start(
            out=out_1[0].rearrange("p c r -> p (c r)").bitcast(I32), in_=y_code[:].bitcast(I32)
        )
        for quad in range(4):
            queue = nc.scalar if quad == 3 else nc.sync
            queue.dma_start(
                out=out_2[0, 4 * quad : 4 * quad + 4, :].bitcast(I32),
                in_=y_scale[32 * quad : 32 * quad + 4, :].bitcast(I32),
            )
